import numpy as np
import ml_dtypes


def mxq(x, axis, fmt="e4m3"):
    dtype, down = {"e4m3": (ml_dtypes.float8_e4m3fn, 7), "e5m2": (ml_dtypes.float8_e5m2, 14)}[fmt]
    v = np.moveaxis(np.asarray(x, np.float32).astype(ml_dtypes.bfloat16).astype(np.float64), axis, -1)
    blocks = v.reshape(v.shape[:-1] + (-1, 32))
    amax = np.abs(blocks).max(-1, keepdims=True)
    byte = np.maximum(np.where(amax > 0, np.frexp(amax)[1] - 1 + 127, 0) - down, 1)
    scale = np.exp2(byte - 127.0)
    codes = (blocks / scale).astype(np.float32).astype(dtype).astype(np.float64)
    return np.moveaxis((codes * scale).reshape(v.shape), -1, axis)


WIDE = False


def mx_kscale(k):
    if not WIDE:
        return np.ones(k)
    levels = np.array([30, -30])
    if k % 512:
        return np.exp2(np.random.permutation(np.resize(levels, k // 32))).repeat(32)
    a = np.empty((k // 512, 16))
    for p in range(k // 512):
        a[p, :8] = np.random.permutation(np.resize(levels, 8))
        for g in range(8):
            far = levels[np.abs(levels - a[p, g]) >= 10]
            a[p, g + 8] = far[np.random.randint(len(far))]
    return np.exp2(a.ravel()).repeat(32)


def f64(x):
    return np.asarray(x).astype(np.float64)


def striped(idx):
    return np.tile(np.asarray(idx).reshape(-1, 16).T, (8, 1)).astype(np.uint16)


def unstriped(offs):
    return offs[:16].T.reshape(-1).astype(np.int64)


def bf(x):
    return np.asarray(x, np.float32).astype(ml_dtypes.bfloat16)


def planes(Y):
    r, m = Y.shape
    b = f64(bf(Y)).reshape(r // 32, 32, m)
    amax = np.abs(b).max(1)
    byte = np.clip(np.where(amax > 0, np.frexp(amax)[1] - 1 + 127 - 7, 1), 1, 254)
    codes = (b * np.exp2(127.0 - byte)[:, None, :]).reshape(r, m).astype(np.float32).astype(ml_dtypes.float8_e4m3fn).view(np.uint8)
    words = codes.reshape(r // 512, 128, 4, m).transpose(0, 1, 3, 2)
    return np.ascontiguousarray(words), np.ascontiguousarray(byte.astype(np.uint8).reshape(r // 512, 16, m))


K, N, T, J = 512, 512, 2048, 512


def setup_inputs():
    n = np.random.standard_normal
    idx = np.random.permutation(T)[:J]
    fj = mx_kscale(J)
    return {
        "xa": (n((K, T))).astype(np.float32),
        "xb": (n((N, T))).astype(np.float32),
        "ra": (np.random.uniform(0.5, 1.5, (1, J)) * fj).astype(np.float32),
        "rb": (np.random.uniform(0.5, 1.5, (1, J)) / fj).astype(np.float32),
        "offs": striped(idx),
    }


def reference(xa, xb, ra, rb, offs):
    idx = unstriped(offs)
    da = (f64(xa)[:, idx] - np.mean(f64(xa)[:, idx], axis=1, keepdims=True)) * f64(ra)
    db = (f64(xb)[:, idx] - np.mean(f64(xb)[:, idx], axis=1, keepdims=True)) * f64(rb)
    ta = da.T
    tb = db.T
    taq = mxq(ta, 0, "e4m3")
    tbq = mxq(tb, 0, "e5m2")
    v = taq.T @ tbq
    y = 0.04 * v
    words, scales = planes(y)
    return y, words, scales

@@ -1,0 +1,203 @@
+from contextlib import ExitStack
+
+import concourse.mybir as mybir
+from concourse.masks import make_identity
+
+K, N, T, J = 512, 512, 2048, 512
+FLOPS = 2 * K * N * J
+
+F32 = mybir.dt.float32
+BF16 = mybir.dt.bfloat16
+I32 = mybir.dt.int32
+U32 = mybir.dt.uint32
+U16 = mybir.dt.uint16
+U8 = mybir.dt.uint8
+E4M3X4 = mybir.dt.float8_e4m3fn_x4
+E5M2X4 = mybir.dt.float8_e5m2_x4
+ALU = mybir.AluOpType
+ACT = mybir.ActivationFunctionType
+
+P = 128
+PACK = 4
+HALF = J // 2
+OUT_SCALE = 0.04
+TILES = 2 * PACK
+LAST = TILES - 1
+HEAD = 64
+SLOT_BYTES = 4 * J
+STAGE_BYTES = 2 * J
+PICKED_BASE = (TILES + 4) * SLOT_BYTES
+
+
+def tile_list_listed_cross_covariance_pl_kernel(tc, xa, xb, ra, rb, offs, out_0, out_1, out_2):
+    nc = tc.nc
+    with ExitStack() as ctx:
+        keep = ctx.enter_context(tc.tile_pool(name="keep", bufs=1))
+        placed = ctx.enter_context(tc.tile_pool(name="placed", bufs=1))
+        psum = ctx.enter_context(tc.psum_pool(name="psum", bufs=1))
+
+        xa_rows = xa.rearrange("(m t) c -> t m c", t=PACK)
+        xb_rows = xb.rearrange("(t m) c -> t m c", t=PACK)
+        sources = [xb_rows[t] for t in range(PACK)] + [xa_rows[t] for t in range(PACK)]
+        windows = [keep.tile([P, T], F32, name=f"window{i}") for i in range(TILES)]
+        offsets = keep.tile([P, J // 16], U16, name="offsets")
+
+        nc.sync.dma_start(windows[0][:], sources[0])
+        nc.sync.dma_start(offsets[:], offs)
+        for i in range(1, TILES):
+            nc.sync.dma_start(windows[i][:], sources[i])
+
+        identity = keep.tile([P, P], F32, name="identity")
+        make_identity(nc, identity[:])
+
+        spread = []
+        for name, r in (("b", rb), ("a", ra)):
+            r_cols = keep.tile([P, PACK], F32, name=f"r_cols_{name}")
+            nc.scalar.dma_start(r_cols[:], r.rearrange("o (p t) -> (o p) t", t=PACK))
+            bank = psum.tile([P, PACK, P], F32, name=f"r_spread_{name}")
+            for t in range(PACK):
+                nc.tensor.transpose(bank[:, t, :], r_cols[:, t : t + 1].to_broadcast([P, P]), identity[:])
+            spread.append(bank)
+
+        b_codes = keep.tile([P, N], U32, name="b_codes", align_bytes=64)
+        b_scales = keep.tile([P, N], U8, name="b_scales", align_bytes=64)
+        a_scales = keep.tile([P, K], U8, name="a_scales", align_bytes=64)
+        y = keep.tile([P, PACK, N], F32, name="y")
+        out_rows = out_0.rearrange("(p t) n -> p t n", t=PACK)
+
+        def gather(i):
+            picked = placed.tile([P, J], F32, name=f"picked{i}", align_bytes=64, offset=PICKED_BASE + i * SLOT_BYTES)
+            for h in range(2):
+                nc.vector.tensor_copy(
+                    picked[:, h * HALF : (h + 1) * HALF],
+                    windows[i][:].indirect(offsets[:, h * HALF // 16 : (h + 1) * HALF // 16]),
+                )
+            return picked
+
+        def head_width(i):
+            return HALF if i == LAST else HEAD
+
+        def head_sum(i, picked):
+            width = head_width(i)
+            part = keep.tile([P, 1], F32, name=f"part{i}")
+            scaled = placed.tile([P, 2 * HALF], F32, name=f"head{i}", align_bytes=64, offset=i * SLOT_BYTES)
+            nc.scalar.activation(
+                scaled[:, :width], picked[:, :width], ACT.Identity, scale=1.0 / (J * (J - width)), accum_out=part[:]
+            )
+            return part
+
+        def average(i, picked, part):
+            width = head_width(i)
+            mean = keep.tile([P, 1], F32, name=f"mean{i}")
+            scaled = keep.tile([P, J], F32, name="scaled", bufs=2)
+            nc.scalar.activation(
+                scaled[:, width:], picked[:, width:], ACT.Identity, bias=part[:], scale=1.0 / J, accum_out=mean[:]
+            )
+            return mean
+
+        def centre(i, picked, mean):
+            r_bank = spread[i // PACK]
+            pairs = placed.tile([P, J], BF16, name=f"pairs{i}", align_bytes=64, offset=(i + 1) * SLOT_BYTES)
+            turned = psum.tile([P, 2, P], F32, name="turned", bufs=2)
+            if i == LAST:
+                for u in range(2):
+                    half = pairs[:, u * HALF : (u + 1) * HALF]
+                    nc.vector.scalar_tensor_tensor(
+                        out=half.rearrange("k (p e) -> k p e", e=2),
+                        in0=picked[:].rearrange("k (p u e) -> k u p e", u=2, e=2)[:, u, :, :],
+                        scalar=mean[:],
+                        in1=r_bank[:].rearrange("k (u e) p -> k u p e", u=2)[:, u, :, :],
+                        op0=ALU.subtract,
+                        op1=ALU.mult,
+                    )
+                    nc.tensor.transpose(turned[:, u, :], half.bitcast(F32), identity[:])
+            else:
+                nc.vector.scalar_tensor_tensor(
+                    out=pairs[:].rearrange("k (p t) -> k p t", t=PACK),
+                    in0=picked[:].rearrange("k (p t) -> k p t", t=PACK),
+                    scalar=mean[:],
+                    in1=r_bank[:].rearrange("k t p -> k p t"),
+                    op0=ALU.subtract,
+                    op1=ALU.mult,
+                )
+                for u in range(2):
+                    nc.tensor.transpose(turned[:, u, :], pairs[:].bitcast(F32)[:, u::2], identity[:])
+            return turned
+
+        def group(i, turned):
+            grouped = placed.tile(
+                [P, J], BF16, name=f"grouped{i}", align_bytes=64, offset=(i + 2) * SLOT_BYTES + STAGE_BYTES
+            )
+            nc.scalar.copy(
+                grouped[:].bitcast(F32).rearrange("p (c u) -> p c u", u=2),
+                turned[:].rearrange("p u c -> p c u"),
+            )
+            return grouped
+
+        def quantise(i, grouped):
+            t = i % PACK
+            cols = slice(t * P, (t + 1) * P)
+            if i < PACK:
+                nc.vector.quantize_mx(out=b_codes[:, cols].bitcast(E5M2X4), scales=b_scales[:, cols], in_=grouped[:])
+                return
+            if i == LAST - 2:
+                a_codes = placed.tile([P, P], U32, name=f"a_codes{t}", align_bytes=64, offset=PICKED_BASE + LAST * SLOT_BYTES)
+            else:
+                a_codes = keep.tile([P, P], U32, name=f"a_codes{t}", align_bytes=64)
+            nc.vector.quantize_mx(out=a_codes[:].bitcast(E4M3X4), scales=a_scales[:, cols], in_=grouped[:])
+            acc = psum.tile([P, N], F32, name=f"acc{t}")
+            nc.tensor.matmul_mx(
+                out=acc[:],
+                lhsT=a_codes[:].bitcast(E4M3X4),
+                lhsT_scale=a_scales[:, cols],
+                rhs=b_codes[:].bitcast(E5M2X4),
+                rhs_scale=b_scales[:],
+                start=True,
+                stop=True,
+            )
+            for h in range(2):
+                n_cols = slice(h * N // 2, (h + 1) * N // 2)
+                nc.scalar.activation(y[:, t, n_cols], acc[:, n_cols], ACT.Copy, scale=OUT_SCALE)
+            nc.sync.dma_start(out_rows[:, t, :], y[:, t, :])
+
+        picked, means, turned, grouped = {}, {}, {}, {}
+        for step in range(TILES + 2):
+            if step < TILES:
+                picked[step] = gather(step)
+                part = head_sum(step, picked[step])
+            if step == LAST:
+                means[step] = average(step, picked[step], part)
+            if step >= 2:
+                grouped[step - 2] = group(step - 2, turned[step - 2])
+            if step < LAST:
+                means[step] = average(step, picked[step], part)
+            if 1 <= step <= TILES:
+                turned[step - 1] = centre(step - 1, picked[step - 1], means[step - 1])
+            if step == TILES:
+                quantise(LAST - 2, grouped[LAST - 2])
+            if step >= 2 and step != LAST:
+                quantise(step - 2, grouped[step - 2])
+
+        y_grouped = placed.tile(
+            [P, PACK * N], BF16, name="y_grouped", align_bytes=64, offset=(LAST + 2) * SLOT_BYTES + STAGE_BYTES
+        )
+        y_view = y_grouped[:].rearrange("p (n t) -> p n t", t=PACK)
+        y_src = y[:].rearrange("p t n -> p n t")
+        nc.vector.tensor_copy(y_view[:, :, 0:2], y_src[:, :, 0:2])
+        y_codes = keep.tile([P, N], U32, name="y_codes", align_bytes=64)
+        y_scales = keep.tile([P, N], U8, name="y_scales", align_bytes=64)
+        words_out = out_1.rearrange("z l c r -> (z l) (c r)").bitcast(I32)
+        scales_out = out_2.rearrange("z q c -> (z q) c").bitcast(I32)
+        halves = [slice(h * N // 2, (h + 1) * N // 2) for h in range(2)]
+        for n_cols in halves:
+            nc.vector.tensor_copy(y_view[:, n_cols, 2:4], y_src[:, n_cols, 2:4])
+        for n_cols in halves:
+            nc.vector.quantize_mx(
+                out=y_codes[:, n_cols].bitcast(E4M3X4),
+                scales=y_scales[:, n_cols],
+                in_=y_grouped[:, n_cols.start * PACK : n_cols.stop * PACK],
+            )
+            nc.sync.dma_start(words_out[:, n_cols], y_codes[:, n_cols].bitcast(I32))
+        for q in range(4):
+            engine = nc.sync if q < 2 else nc.scalar
+            engine.dma_start(scales_out[4 * q : 4 * q + 4, :], y_scales[:].bitcast(I32)[32 * q : 32 * q + 4, :])

@@ -19,14 +19,19 @@ ACT = mybir.ActivationFunctionType
 
 P = 128
 PACK = 4
-HALF = J // 2
 OUT_SCALE = 0.04
-TILES = 2 * PACK
-LAST = TILES - 1
+WINDOWS = 2 * PACK
+LAST = WINDOWS - 1
+HALF = J // 2
+LIST_ROWS = 16
 HEAD = 64
+QUARTER = N // 4
+
 SLOT_BYTES = 4 * J
-STAGE_BYTES = 2 * J
-PICKED_BASE = (TILES + 4) * SLOT_BYTES
+HALF_SLOT_BYTES = SLOT_BYTES // 2
+Y_GROUPED_AT = (LAST + 2) * SLOT_BYTES + HALF_SLOT_BYTES
+PICKED_AT = (WINDOWS + 4) * SLOT_BYTES
+Y_LOW_AT = PICKED_AT + WINDOWS * SLOT_BYTES
 
 
 def tile_list_listed_cross_covariance_pl_kernel(tc, xa, xb, ra, rb, offs, out_0, out_1, out_2):
@@ -39,115 +44,105 @@ def tile_list_listed_cross_covariance_pl_kernel(tc, xa, xb, ra, rb, offs, out_0,
         xa_rows = xa.rearrange("(m t) c -> t m c", t=PACK)
         xb_rows = xb.rearrange("(t m) c -> t m c", t=PACK)
         sources = [xb_rows[t] for t in range(PACK)] + [xa_rows[t] for t in range(PACK)]
-        windows = [keep.tile([P, T], F32, name=f"window{i}") for i in range(TILES)]
-        offsets = keep.tile([P, J // 16], U16, name="offsets")
-
+        windows = [keep.tile([P, T], F32, name=f"window{i}") for i in range(WINDOWS)]
+        offsets = keep.tile([P, J // LIST_ROWS], U16, name="offsets")
         nc.sync.dma_start(windows[0][:], sources[0])
         nc.sync.dma_start(offsets[:], offs)
-        for i in range(1, TILES):
+        for i in range(1, WINDOWS):
             nc.sync.dma_start(windows[i][:], sources[i])
 
         identity = keep.tile([P, P], F32, name="identity")
         make_identity(nc, identity[:])
 
-        spread = []
+        weights = []
         for name, r in (("b", rb), ("a", ra)):
             r_cols = keep.tile([P, PACK], F32, name=f"r_cols_{name}")
             nc.scalar.dma_start(r_cols[:], r.rearrange("o (p t) -> (o p) t", t=PACK))
-            bank = psum.tile([P, PACK, P], F32, name=f"r_spread_{name}")
+            bank = psum.tile([P, PACK, P], F32, name=f"weights_{name}")
             for t in range(PACK):
                 nc.tensor.transpose(bank[:, t, :], r_cols[:, t : t + 1].to_broadcast([P, P]), identity[:])
-            spread.append(bank)
+            weights.append(bank)
 
         b_codes = keep.tile([P, N], U32, name="b_codes", align_bytes=64)
         b_scales = keep.tile([P, N], U8, name="b_scales", align_bytes=64)
         a_scales = keep.tile([P, K], U8, name="a_scales", align_bytes=64)
-        y = keep.tile([P, PACK, N], F32, name="y")
         out_rows = out_0.rearrange("(p t) n -> p t n", t=PACK)
 
         def gather(i):
-            picked = placed.tile([P, J], F32, name=f"picked{i}", align_bytes=64, offset=PICKED_BASE + i * SLOT_BYTES)
+            picked = placed.tile([P, J], F32, name=f"picked{i}", align_bytes=64, offset=PICKED_AT + i * SLOT_BYTES)
             for h in range(2):
-                nc.vector.tensor_copy(
-                    picked[:, h * HALF : (h + 1) * HALF],
-                    windows[i][:].indirect(offsets[:, h * HALF // 16 : (h + 1) * HALF // 16]),
-                )
+                entries = offsets[:, h * HALF // LIST_ROWS : (h + 1) * HALF // LIST_ROWS]
+                nc.vector.tensor_copy(picked[:, h * HALF : (h + 1) * HALF], windows[i][:].indirect(entries))
             return picked
 
-        def head_width(i):
-            return HALF if i == LAST else HEAD
-
-        def head_sum(i, picked):
-            width = head_width(i)
-            part = keep.tile([P, 1], F32, name=f"part{i}")
-            scaled = placed.tile([P, 2 * HALF], F32, name=f"head{i}", align_bytes=64, offset=i * SLOT_BYTES)
+        def head_sum(picked, i, width):
+            share = keep.tile([P, 1], F32, name=f"share{i}")
+            scratch = placed.tile([P, J], F32, name=f"head_scratch{i}", align_bytes=64, offset=i * SLOT_BYTES)
             nc.scalar.activation(
-                scaled[:, :width], picked[:, :width], ACT.Identity, scale=1.0 / (J * (J - width)), accum_out=part[:]
+                scratch[:, :width], picked[:, :width], ACT.Identity, scale=1.0 / (J * (J - width)), accum_out=share[:]
             )
-            return part
+            return share
 
-        def average(i, picked, part):
-            width = head_width(i)
+        def row_mean(picked, i, width, share, scratch):
             mean = keep.tile([P, 1], F32, name=f"mean{i}")
-            scaled = keep.tile([P, J], F32, name="scaled", bufs=2)
             nc.scalar.activation(
-                scaled[:, width:], picked[:, width:], ACT.Identity, bias=part[:], scale=1.0 / J, accum_out=mean[:]
+                scratch[:, width:], picked[:, width:], ACT.Identity, bias=share[:], scale=1.0 / J, accum_out=mean[:]
             )
             return mean
 
-        def centre(i, picked, mean):
-            r_bank = spread[i // PACK]
-            pairs = placed.tile([P, J], BF16, name=f"pairs{i}", align_bytes=64, offset=(i + 1) * SLOT_BYTES)
+        def centred_tile(i):
+            return placed.tile([P, J], BF16, name=f"centred{i}", align_bytes=64, offset=(i + 1) * SLOT_BYTES)
+
+        def centre(picked, i, mean):
+            centred = centred_tile(i)
             turned = psum.tile([P, 2, P], F32, name="turned", bufs=2)
-            if i == LAST:
-                for u in range(2):
-                    half = pairs[:, u * HALF : (u + 1) * HALF]
-                    nc.vector.scalar_tensor_tensor(
-                        out=half.rearrange("k (p e) -> k p e", e=2),
-                        in0=picked[:].rearrange("k (p u e) -> k u p e", u=2, e=2)[:, u, :, :],
-                        scalar=mean[:],
-                        in1=r_bank[:].rearrange("k (u e) p -> k u p e", u=2)[:, u, :, :],
-                        op0=ALU.subtract,
-                        op1=ALU.mult,
-                    )
-                    nc.tensor.transpose(turned[:, u, :], half.bitcast(F32), identity[:])
-            else:
+            nc.vector.scalar_tensor_tensor(
+                out=centred[:].rearrange("m (p t) -> m p t", t=PACK),
+                in0=picked[:].rearrange("m (p t) -> m p t", t=PACK),
+                scalar=mean[:],
+                in1=weights[i // PACK][:].rearrange("m t p -> m p t"),
+                op0=ALU.subtract,
+                op1=ALU.mult,
+            )
+            for u in range(2):
+                nc.tensor.transpose(turned[:, u, :], centred[:].bitcast(F32)[:, u::2], identity[:])
+            return turned
+
+        def centre_by_halves(picked, i, mean):
+            centred = centred_tile(i)
+            turned = psum.tile([P, 2, P], F32, name="turned", bufs=2)
+            for u in range(2):
+                words = centred[:, u * HALF : (u + 1) * HALF]
                 nc.vector.scalar_tensor_tensor(
-                    out=pairs[:].rearrange("k (p t) -> k p t", t=PACK),
-                    in0=picked[:].rearrange("k (p t) -> k p t", t=PACK),
+                    out=words.rearrange("m (p e) -> m p e", e=2),
+                    in0=picked[:].rearrange("m (p u e) -> m u p e", u=2, e=2)[:, u, :, :],
                     scalar=mean[:],
-                    in1=r_bank[:].rearrange("k t p -> k p t"),
+                    in1=weights[i // PACK][:].rearrange("m (u e) p -> m u p e", u=2)[:, u, :, :],
                     op0=ALU.subtract,
                     op1=ALU.mult,
                 )
-                for u in range(2):
-                    nc.tensor.transpose(turned[:, u, :], pairs[:].bitcast(F32)[:, u::2], identity[:])
+                nc.tensor.transpose(turned[:, u, :], words.bitcast(F32), identity[:])
             return turned
 
-        def group(i, turned):
+        def group(turned, i):
             grouped = placed.tile(
-                [P, J], BF16, name=f"grouped{i}", align_bytes=64, offset=(i + 2) * SLOT_BYTES + STAGE_BYTES
+                [P, J], BF16, name=f"grouped{i}", align_bytes=64, offset=(i + 2) * SLOT_BYTES + HALF_SLOT_BYTES
             )
             nc.scalar.copy(
-                grouped[:].bitcast(F32).rearrange("p (c u) -> p c u", u=2),
-                turned[:].rearrange("p u c -> p c u"),
+                grouped[:].bitcast(F32).rearrange("p (m u) -> p m u", u=2), turned[:].rearrange("p u m -> p m u")
             )
             return grouped
 
-        def quantise(i, grouped):
-            t = i % PACK
+        def quantise_b(grouped, t):
             cols = slice(t * P, (t + 1) * P)
-            if i < PACK:
-                nc.vector.quantize_mx(out=b_codes[:, cols].bitcast(E5M2X4), scales=b_scales[:, cols], in_=grouped[:])
-                return
-            if i == LAST - 2:
-                a_codes = placed.tile([P, P], U32, name=f"a_codes{t}", align_bytes=64, offset=PICKED_BASE + LAST * SLOT_BYTES)
-            else:
-                a_codes = keep.tile([P, P], U32, name=f"a_codes{t}", align_bytes=64)
+            nc.vector.quantize_mx(out=b_codes[:, cols].bitcast(E5M2X4), scales=b_scales[:, cols], in_=grouped[:])
+
+        def multiply(grouped, t, a_codes):
+            cols = slice(t * P, (t + 1) * P)
             nc.vector.quantize_mx(out=a_codes[:].bitcast(E4M3X4), scales=a_scales[:, cols], in_=grouped[:])
-            acc = psum.tile([P, N], F32, name=f"acc{t}")
+            v = psum.tile([P, N], F32, name=f"v{t}")
             nc.tensor.matmul_mx(
-                out=acc[:],
+                out=v[:],
                 lhsT=a_codes[:].bitcast(E4M3X4),
                 lhsT_scale=a_scales[:, cols],
                 rhs=b_codes[:].bitcast(E5M2X4),
@@ -155,49 +150,72 @@ def tile_list_listed_cross_covariance_pl_kernel(tc, xa, xb, ra, rb, offs, out_0,
                 start=True,
                 stop=True,
             )
-            for h in range(2):
-                n_cols = slice(h * N // 2, (h + 1) * N // 2)
-                nc.scalar.activation(y[:, t, n_cols], acc[:, n_cols], ACT.Copy, scale=OUT_SCALE)
-            nc.sync.dma_start(out_rows[:, t, :], y[:, t, :])
+            return v
+
+        def scale_and_store(v, t, y_rows, pieces):
+            for cols in pieces:
+                nc.scalar.activation(y_rows[:, cols], v[:, cols], ACT.Copy, scale=OUT_SCALE)
+            nc.sync.dma_start(out_rows[:, t, :], y_rows)
+
+        def own_codes(t):
+            return keep.tile([P, P], U32, name=f"a_codes{t}", align_bytes=64)
 
         picked, means, turned, grouped = {}, {}, {}, {}
-        for step in range(TILES + 2):
-            if step < TILES:
-                picked[step] = gather(step)
-                part = head_sum(step, picked[step])
-            if step == LAST:
-                means[step] = average(step, picked[step], part)
-            if step >= 2:
-                grouped[step - 2] = group(step - 2, turned[step - 2])
-            if step < LAST:
-                means[step] = average(step, picked[step], part)
-            if 1 <= step <= TILES:
-                turned[step - 1] = centre(step - 1, picked[step - 1], means[step - 1])
-            if step == TILES:
-                quantise(LAST - 2, grouped[LAST - 2])
-            if step >= 2 and step != LAST:
-                quantise(step - 2, grouped[step - 2])
+        for i in range(LAST):
+            picked[i] = gather(i)
+            share = head_sum(picked[i], i, HEAD)
+            if i >= 2:
+                grouped[i - 2] = group(turned[i - 2], i - 2)
+            scratch = keep.tile([P, J], F32, name="mean_scratch", bufs=2)
+            means[i] = row_mean(picked[i], i, HEAD, share, scratch)
+            if i >= 1:
+                turned[i - 1] = centre(picked[i - 1], i - 1, means[i - 1])
+            if 2 <= i < PACK + 2:
+                quantise_b(grouped[i - 2], i - 2)
+        first_v = multiply(grouped[PACK], 0, own_codes(0))
 
-        y_grouped = placed.tile(
-            [P, PACK * N], BF16, name="y_grouped", align_bytes=64, offset=(LAST + 2) * SLOT_BYTES + STAGE_BYTES
-        )
-        y_view = y_grouped[:].rearrange("p (n t) -> p n t", t=PACK)
-        y_src = y[:].rearrange("p t n -> p n t")
-        nc.vector.tensor_copy(y_view[:, :, 0:2], y_src[:, :, 0:2])
+        picked[LAST] = gather(LAST)
+        share = head_sum(picked[LAST], LAST, HALF)
+        scratch = placed.tile([P, J], F32, name="last_mean_scratch", align_bytes=64, offset=Y_LOW_AT)
+        means[LAST] = row_mean(picked[LAST], LAST, HALF, share, scratch)
+        grouped[LAST - 2] = group(turned[LAST - 2], LAST - 2)
+
+        whole = [slice(0, N)]
+        y_low = placed.tile([P, 2, N], F32, name="y_low", align_bytes=64, offset=Y_LOW_AT)
+        scale_and_store(first_v, 0, y_low[:, 0, :], whole)
+        turned[LAST - 1] = centre(picked[LAST - 1], LAST - 1, means[LAST - 1])
+        turned[LAST] = centre_by_halves(picked[LAST], LAST, means[LAST])
+        for i in (LAST - 1, LAST):
+            grouped[i] = group(turned[i], i)
+
+        late_codes = placed.tile([P, P], U32, name="a_codes1", align_bytes=64, offset=PICKED_AT + LAST * SLOT_BYTES)
+        scale_and_store(multiply(grouped[PACK + 1], 1, late_codes), 1, y_low[:, 1, :], whole)
+        third_v = multiply(grouped[PACK + 2], 2, own_codes(2))
+        y_high = keep.tile([P, 2, N], F32, name="y_high")
+        scale_and_store(third_v, 2, y_high[:, 0, :], whole)
+        quarters = [slice(q * QUARTER, (q + 1) * QUARTER) for q in range(4)]
+        last_v = multiply(grouped[LAST], 3, own_codes(3))
+        scale_and_store(last_v, 3, y_high[:, 1, :], [quarters[q] for q in (0, 1, 3, 2)])
+
+        y_grouped = placed.tile([P, PACK * N], BF16, name="y_grouped", align_bytes=64, offset=Y_GROUPED_AT)
+        y_by_column = y_grouped[:].rearrange("p (n t) -> p n t", t=PACK)
+        high_by_column = y_high[:].rearrange("p t n -> p n t")
+        nc.vector.tensor_copy(y_by_column[:, :, 0:2], y_low[:].rearrange("p t n -> p n t"))
+        for cols in quarters[:3]:
+            nc.vector.tensor_copy(y_by_column[:, cols, 2:4], high_by_column[:, cols, :])
+        nc.scalar.copy(y_by_column[:, quarters[3], 2:4], high_by_column[:, quarters[3], :])
+
         y_codes = keep.tile([P, N], U32, name="y_codes", align_bytes=64)
         y_scales = keep.tile([P, N], U8, name="y_scales", align_bytes=64)
         words_out = out_1.rearrange("z l c r -> (z l) (c r)").bitcast(I32)
         scales_out = out_2.rearrange("z q c -> (z q) c").bitcast(I32)
-        halves = [slice(h * N // 2, (h + 1) * N // 2) for h in range(2)]
-        for n_cols in halves:
-            nc.vector.tensor_copy(y_view[:, n_cols, 2:4], y_src[:, n_cols, 2:4])
-        for n_cols in halves:
+        for cols in (slice(0, N // 2), slice(N // 2, N)):
             nc.vector.quantize_mx(
-                out=y_codes[:, n_cols].bitcast(E4M3X4),
-                scales=y_scales[:, n_cols],
-                in_=y_grouped[:, n_cols.start * PACK : n_cols.stop * PACK],
+                out=y_codes[:, cols].bitcast(E4M3X4),
+                scales=y_scales[:, cols],
+                in_=y_grouped[:, cols.start * PACK : cols.stop * PACK],
             )
-            nc.sync.dma_start(words_out[:, n_cols], y_codes[:, n_cols].bitcast(I32))
+            nc.sync.dma_start(words_out[:, cols], y_codes[:, cols].bitcast(I32))
         for q in range(4):
-            engine = nc.sync if q < 2 else nc.scalar
-            engine.dma_start(scales_out[4 * q : 4 * q + 4, :], y_scales[:].bitcast(I32)[32 * q : 32 * q + 4, :])
+            queue = nc.sync if q < 2 else nc.scalar
+            queue.dma_start(scales_out[4 * q : 4 * q + 4, :], y_scales[:].bitcast(I32)[32 * q : 32 * q + 4, :])

from contextlib import ExitStack

import concourse.mybir as mybir
from concourse.masks import make_identity

K, N, T, J = 512, 512, 2048, 512
FLOPS = 2 * K * N * J

F32 = mybir.dt.float32
BF16 = mybir.dt.bfloat16
I32 = mybir.dt.int32
U32 = mybir.dt.uint32
U16 = mybir.dt.uint16
U8 = mybir.dt.uint8
E4M3X4 = mybir.dt.float8_e4m3fn_x4
E5M2X4 = mybir.dt.float8_e5m2_x4
ALU = mybir.AluOpType
ACT = mybir.ActivationFunctionType

P = 128
PACK = 4
OUT_SCALE = 0.04
WINDOWS = 2 * PACK
LAST = WINDOWS - 1
HALF = J // 2
LIST_ROWS = 16
HEAD = 64
QUARTER = N // 4

SLOT_BYTES = 4 * J
HALF_SLOT_BYTES = SLOT_BYTES // 2
Y_GROUPED_AT = (LAST + 2) * SLOT_BYTES + HALF_SLOT_BYTES
PICKED_AT = (WINDOWS + 4) * SLOT_BYTES
Y_LOW_AT = PICKED_AT + WINDOWS * SLOT_BYTES


def tile_list_listed_cross_covariance_pl_kernel(tc, xa, xb, ra, rb, offs, out_0, out_1, out_2):
    nc = tc.nc
    with ExitStack() as ctx:
        keep = ctx.enter_context(tc.tile_pool(name="keep", bufs=1))
        placed = ctx.enter_context(tc.tile_pool(name="placed", bufs=1))
        psum = ctx.enter_context(tc.psum_pool(name="psum", bufs=1))

        xa_rows = xa.rearrange("(m t) c -> t m c", t=PACK)
        xb_rows = xb.rearrange("(t m) c -> t m c", t=PACK)
        sources = [xb_rows[t] for t in range(PACK)] + [xa_rows[t] for t in range(PACK)]
        windows = [keep.tile([P, T], F32, name=f"window{i}") for i in range(WINDOWS)]
        offsets = keep.tile([P, J // LIST_ROWS], U16, name="offsets")
        nc.sync.dma_start(windows[0][:], sources[0])
        nc.sync.dma_start(offsets[:], offs)
        for i in range(1, WINDOWS):
            nc.sync.dma_start(windows[i][:], sources[i])

        identity = keep.tile([P, P], F32, name="identity")
        make_identity(nc, identity[:])

        weights = []
        for name, r in (("b", rb), ("a", ra)):
            r_cols = keep.tile([P, PACK], F32, name=f"r_cols_{name}")
            nc.scalar.dma_start(r_cols[:], r.rearrange("o (p t) -> (o p) t", t=PACK))
            bank = psum.tile([P, PACK, P], F32, name=f"weights_{name}")
            for t in range(PACK):
                nc.tensor.transpose(bank[:, t, :], r_cols[:, t : t + 1].to_broadcast([P, P]), identity[:])
            weights.append(bank)

        b_codes = keep.tile([P, N], U32, name="b_codes", align_bytes=64)
        b_scales = keep.tile([P, N], U8, name="b_scales", align_bytes=64)
        a_scales = keep.tile([P, K], U8, name="a_scales", align_bytes=64)
        out_rows = out_0.rearrange("(p t) n -> p t n", t=PACK)

        def gather(i):
            picked = placed.tile([P, J], F32, name=f"picked{i}", align_bytes=64, offset=PICKED_AT + i * SLOT_BYTES)
            for h in range(2):
                entries = offsets[:, h * HALF // LIST_ROWS : (h + 1) * HALF // LIST_ROWS]
                nc.vector.tensor_copy(picked[:, h * HALF : (h + 1) * HALF], windows[i][:].indirect(entries))
            return picked

        def head_sum(picked, i, width):
            share = keep.tile([P, 1], F32, name=f"share{i}")
            scratch = placed.tile([P, J], F32, name=f"head_scratch{i}", align_bytes=64, offset=i * SLOT_BYTES)
            nc.scalar.activation(
                scratch[:, :width], picked[:, :width], ACT.Identity, scale=1.0 / (J * (J - width)), accum_out=share[:]
            )
            return share

        def row_mean(picked, i, width, share, scratch):
            mean = keep.tile([P, 1], F32, name=f"mean{i}")
            nc.scalar.activation(
                scratch[:, width:], picked[:, width:], ACT.Identity, bias=share[:], scale=1.0 / J, accum_out=mean[:]
            )
            return mean

        def centred_tile(i):
            return placed.tile([P, J], BF16, name=f"centred{i}", align_bytes=64, offset=(i + 1) * SLOT_BYTES)

        def centre(picked, i, mean):
            centred = centred_tile(i)
            turned = psum.tile([P, 2, P], F32, name="turned", bufs=2)
            nc.vector.scalar_tensor_tensor(
                out=centred[:].rearrange("m (p t) -> m p t", t=PACK),
                in0=picked[:].rearrange("m (p t) -> m p t", t=PACK),
                scalar=mean[:],
                in1=weights[i // PACK][:].rearrange("m t p -> m p t"),
                op0=ALU.subtract,
                op1=ALU.mult,
            )
            for u in range(2):
                nc.tensor.transpose(turned[:, u, :], centred[:].bitcast(F32)[:, u::2], identity[:])
            return turned

        def centre_by_halves(picked, i, mean):
            centred = centred_tile(i)
            turned = psum.tile([P, 2, P], F32, name="turned", bufs=2)
            for u in range(2):
                words = centred[:, u * HALF : (u + 1) * HALF]
                nc.vector.scalar_tensor_tensor(
                    out=words.rearrange("m (p e) -> m p e", e=2),
                    in0=picked[:].rearrange("m (p u e) -> m u p e", u=2, e=2)[:, u, :, :],
                    scalar=mean[:],
                    in1=weights[i // PACK][:].rearrange("m (u e) p -> m u p e", u=2)[:, u, :, :],
                    op0=ALU.subtract,
                    op1=ALU.mult,
                )
                nc.tensor.transpose(turned[:, u, :], words.bitcast(F32), identity[:])
            return turned

        def group(turned, i):
            grouped = placed.tile(
                [P, J], BF16, name=f"grouped{i}", align_bytes=64, offset=(i + 2) * SLOT_BYTES + HALF_SLOT_BYTES
            )
            nc.scalar.copy(
                grouped[:].bitcast(F32).rearrange("p (m u) -> p m u", u=2), turned[:].rearrange("p u m -> p m u")
            )
            return grouped

        def quantise_b(grouped, t):
            cols = slice(t * P, (t + 1) * P)
            nc.vector.quantize_mx(out=b_codes[:, cols].bitcast(E5M2X4), scales=b_scales[:, cols], in_=grouped[:])

        def multiply(grouped, t, a_codes):
            cols = slice(t * P, (t + 1) * P)
            nc.vector.quantize_mx(out=a_codes[:].bitcast(E4M3X4), scales=a_scales[:, cols], in_=grouped[:])
            v = psum.tile([P, N], F32, name=f"v{t}")
            nc.tensor.matmul_mx(
                out=v[:],
                lhsT=a_codes[:].bitcast(E4M3X4),
                lhsT_scale=a_scales[:, cols],
                rhs=b_codes[:].bitcast(E5M2X4),
                rhs_scale=b_scales[:],
                start=True,
                stop=True,
            )
            return v

        def scale_and_store(v, t, y_rows, pieces):
            for cols in pieces:
                nc.scalar.activation(y_rows[:, cols], v[:, cols], ACT.Copy, scale=OUT_SCALE)
            nc.sync.dma_start(out_rows[:, t, :], y_rows)

        def own_codes(t):
            return keep.tile([P, P], U32, name=f"a_codes{t}", align_bytes=64)

        picked, means, turned, grouped = {}, {}, {}, {}
        for i in range(LAST):
            picked[i] = gather(i)
            share = head_sum(picked[i], i, HEAD)
            if i >= 2:
                grouped[i - 2] = group(turned[i - 2], i - 2)
            scratch = keep.tile([P, J], F32, name="mean_scratch", bufs=2)
            means[i] = row_mean(picked[i], i, HEAD, share, scratch)
            if i >= 1:
                turned[i - 1] = centre(picked[i - 1], i - 1, means[i - 1])
            if 2 <= i < PACK + 2:
                quantise_b(grouped[i - 2], i - 2)
        first_v = multiply(grouped[PACK], 0, own_codes(0))

        picked[LAST] = gather(LAST)
        share = head_sum(picked[LAST], LAST, HALF)
        scratch = placed.tile([P, J], F32, name="last_mean_scratch", align_bytes=64, offset=Y_LOW_AT)
        means[LAST] = row_mean(picked[LAST], LAST, HALF, share, scratch)
        grouped[LAST - 2] = group(turned[LAST - 2], LAST - 2)

        whole = [slice(0, N)]
        y_low = placed.tile([P, 2, N], F32, name="y_low", align_bytes=64, offset=Y_LOW_AT)
        scale_and_store(first_v, 0, y_low[:, 0, :], whole)
        turned[LAST - 1] = centre(picked[LAST - 1], LAST - 1, means[LAST - 1])
        turned[LAST] = centre_by_halves(picked[LAST], LAST, means[LAST])
        for i in (LAST - 1, LAST):
            grouped[i] = group(turned[i], i)

        late_codes = placed.tile([P, P], U32, name="a_codes1", align_bytes=64, offset=PICKED_AT + LAST * SLOT_BYTES)
        scale_and_store(multiply(grouped[PACK + 1], 1, late_codes), 1, y_low[:, 1, :], whole)
        third_v = multiply(grouped[PACK + 2], 2, own_codes(2))
        y_high = keep.tile([P, 2, N], F32, name="y_high")
        scale_and_store(third_v, 2, y_high[:, 0, :], whole)
        quarters = [slice(q * QUARTER, (q + 1) * QUARTER) for q in range(4)]
        last_v = multiply(grouped[LAST], 3, own_codes(3))
        scale_and_store(last_v, 3, y_high[:, 1, :], [quarters[q] for q in (0, 1, 3, 2)])

        y_grouped = placed.tile([P, PACK * N], BF16, name="y_grouped", align_bytes=64, offset=Y_GROUPED_AT)
        y_by_column = y_grouped[:].rearrange("p (n t) -> p n t", t=PACK)
        high_by_column = y_high[:].rearrange("p t n -> p n t")
        nc.vector.tensor_copy(y_by_column[:, :, 0:2], y_low[:].rearrange("p t n -> p n t"))
        for cols in quarters[:3]:
            nc.vector.tensor_copy(y_by_column[:, cols, 2:4], high_by_column[:, cols, :])
        nc.scalar.copy(y_by_column[:, quarters[3], 2:4], high_by_column[:, quarters[3], :])

        y_codes = keep.tile([P, N], U32, name="y_codes", align_bytes=64)
        y_scales = keep.tile([P, N], U8, name="y_scales", align_bytes=64)
        words_out = out_1.rearrange("z l c r -> (z l) (c r)").bitcast(I32)
        scales_out = out_2.rearrange("z q c -> (z q) c").bitcast(I32)
        for cols in (slice(0, N // 2), slice(N // 2, N)):
            nc.vector.quantize_mx(
                out=y_codes[:, cols].bitcast(E4M3X4),
                scales=y_scales[:, cols],
                in_=y_grouped[:, cols.start * PACK : cols.stop * PACK],
            )
            nc.sync.dma_start(words_out[:, cols], y_codes[:, cols].bitcast(I32))
        for q in range(4):
            queue = nc.sync if q < 2 else nc.scalar
            queue.dma_start(scales_out[4 * q : 4 * q + 4, :], y_scales[:].bitcast(I32)[32 * q : 32 * q + 4, :])
